import numpy as np, ml_dtypes
CORES = [50,52,122,124]
N = 4
S, B = 8, 128
def setup_inputs(rng):
    a = (rng.standard_normal((128, 128), dtype=np.float32) / 8).astype(ml_dtypes.bfloat16)
    return {"x": (rng.standard_normal((N, 128, S * B), dtype=np.float32) / 2).astype(ml_dtypes.bfloat16), "a": np.broadcast_to(a, (N, 128, 128)).copy()}
def reference(x, a):
    X, A = x.astype(np.float64), a.astype(np.float64)
    y = np.zeros((N, 128, S * B)); h = np.zeros((128, B))
    for r in range(N):
        for s in range(S):
            h = np.tanh(A[r].T @ h + X[r][:, B * s:B * s + B])
            y[r][:, B * s:B * s + B] = h
    return {"y": y.astype(ml_dtypes.bfloat16)}

@@ -1,0 +1,217 @@
+from concourse.mybir import AluOpType, ActivationFunctionType
+
+S, B, H = 8, 128, 64
+XCH = [4, 4]
+YCH = [4, 4]
+NB = 4
+
+SCRATCH = {
+    "xs": ("sbuf", [128, S * B], "bfloat16"),
+    "xr": ("sbuf", [128, S * B], "bfloat16"),
+    "ys": ("sbuf", [128, S * B], "bfloat16"),
+    "hs": ("sbuf", [128, S * B], "bfloat16"),
+    "hl": ("sbuf", [128, B], "bfloat16"),
+    "aw": ("sbuf", [128, 128], "bfloat16"),
+    "one": ("sbuf", [128, 128], "bfloat16"),
+    "idn": ("sbuf", [128, 128], "bfloat16"),
+    "z0": ("sbuf", [128, H], "float32"),
+    "z1": ("sbuf", [128, H], "float32"),
+}
+for _i in range(2 * NB):
+    SCRATCH["p%d" % _i] = ("psum", [128, 512], "float32")
+
+SEMAPHORES = ["lx0", "lx1", "la", "one", "idn", "xa0", "xa1", "hi0", "hi1",
+              "m0", "m1", "z0", "z1", "h0", "h1", "snd", "st"]
+
+
+def spans(ch):
+    out, s0 = [], 0
+    for n in ch:
+        out.append((s0, n))
+        s0 += n
+    return out
+
+
+def rank_program(g, core, T, topo):
+    if T.rank_of(core) is None:
+        return
+    c0, c1, c2, c3 = T.cores
+    if not (topo.may_write(c0, c2) and topo.may_write(c0, c3)):
+        raise ValueError("rank 0's core must be allowed to write to ranks 2 and 3")
+    sem = T.sem
+    pe, act, dv, sy = g.tensor, g.scalar, g.vector, g.sync
+    tot = {}
+    cm, cz, ch = [0, 0], [0, 0], [0, 0]
+
+    def note(name, n):
+        tot[name] = tot.get(name, 0) + n
+
+    def nat(buf, s, b):
+        return buf[:, B * s + H * b:B * s + H * b + H]
+
+    def cols(buf, s0, n):
+        return buf[:, B * s0:B * (s0 + n)]
+
+    def bank(b, idx):
+        return T["p%d" % (NB * b + idx % NB)][:, 0:H]
+
+    def bits(m):
+        return bin(m).count("1")
+
+    def send(dst, out_ap, in_ap, rsem, mask):
+        rid, pid, se = topo.addr(dst)
+        g.remote_dma(out_ap=out_ap, in_ap=in_ap, remote_sem=sem[rsem], local_sem=sem.snd,
+                     pid=pid, routing_id=rid, dma_engine_mask=mask)
+        note("snd", bits(mask))
+
+    def load_x(chunks):
+        for k, (s0, n) in enumerate(spans(chunks)):
+            sy.dma_start(cols(T.xs, s0, n), cols(T.x, s0, n)).then_inc(sem["lx%d" % k], 16)
+            note("lx%d" % k, 16)
+
+    def load_a():
+        sy.dma_start(T.aw[:], T.a[:]).then_inc(sem.la, 16)
+        note("la", 16)
+
+    def make_identity():
+        g.wait_ge(sem.one, 1)
+        g.affine_select(T.idn[:], T.one[:], [[-1, 128]], AluOpType.is_equal, 0.0, 0, 1).then_inc(sem.idn, 1)
+        note("idn", 1)
+
+    def tanh(b, out, in_):
+        act.activation(out, in_, ActivationFunctionType.Tanh).then_inc(sem["h%d" % b], 1)
+        ch[b] += 1
+
+    def xpart(b, idx, x):
+        pe.matmul(bank(b, idx), T.idn[:], x, True, False)
+
+    def step(b, idx, x, rhs, out, p, wait=None):
+        ps = bank(b, idx)
+        if wait is None:
+            pe.wait_ge(sem["h%d" % b], ch[b])
+        else:
+            pe.wait_ge(sem[wait], tot[wait])
+        pe.matmul(ps, T.aw[:], rhs, not p, True).then_inc(sem["m%d" % b], 1)
+        cm[b] += 1
+        if p:
+            act.wait_ge(sem["m%d" % b], cm[b])
+            tanh(b, out, ps)
+        else:
+            z = T["z%d" % b][:]
+            dv.wait_ge(sem["m%d" % b], cm[b])
+            dv.tensor_tensor(z, ps, x, AluOpType.add).then_inc(sem["z%d" % b], 1)
+            cz[b] += 1
+            act.wait_ge(sem["z%d" % b], cz[b])
+            tanh(b, out, z)
+
+    def is_p(i):
+        return i < NB or (i - NB) % 3 == 2
+
+    def chain(xb, ob, prev, first):
+        n = len(xb)
+        x = [[nat(u, s, b) for b in (0, 1)] for u, s in xb]
+        o = [[nat(u, s, b) for b in (0, 1)] for u, s in ob]
+        for i in range(min(NB, n)):
+            for b in (0, 1):
+                xpart(b, i, x[i][b])
+        pe.wait_ge(sem.la, 16)
+        for i in range(n):
+            for b in (0, 1):
+                step(b, i, x[i][b], prev[b], o[i][b], is_p(i), first[b] if (i == 0 and first) else None)
+                prev[b] = o[i][b]
+            if NB <= i + 2 < n and is_p(i + 2):
+                xpart(0, i + 2, x[i + 2][0])
+            if NB <= i + 1 < n and is_p(i + 1):
+                xpart(1, i + 1, x[i + 1][1])
+
+    def store(base, chunks):
+        for s0, n in spans(chunks):
+            for b in (0, 1):
+                sy.wait_ge(sem["h%d" % b], base + s0 + n)
+            sy.dma_start(cols(T.y, s0, n), cols(T.ys, s0, n)).then_inc(sem.st, 16)
+            note("st", 16)
+
+    dv.memset(T.one[:], 1.0).then_inc(sem.one, 1)
+    note("one", 1)
+    far = topo.mask(c0, c3) & topo.mask(c0, c2) & topo.mask(c0, c1)
+
+    if core == c0:
+        xin = bits(topo.mask(c1, c0))
+        load_x([1, 7])
+        load_a()
+        make_identity()
+        act.wait_ge(sem.lx0, 16)
+        for b in (0, 1):
+            tanh(b, nat(T.ys, 0, b), nat(T.xs, 0, b))
+        pe.wait_ge(sem.idn, 1)
+        pe.wait_ge(sem.lx1, 16)
+        dv.wait_ge(sem.lx1, 16)
+        chain([(T.xs, s) for s in range(1, S)], [(T.ys, s) for s in range(1, S)],
+              [nat(T.ys, 0, b) for b in (0, 1)], None)
+        for b in (0, 1):
+            g.wait_ge(sem["h%d" % b], S)
+        send(c1, T.hl[:], cols(T.ys, S - 1, 1), "hi0", far)
+        starts = {s0: k for k, (s0, n) in enumerate(spans(XCH))}
+        for k in range(len(XCH)):
+            note("xa%d" % k, xin)
+        for b in (0, 1):
+            prev = nat(T.ys, S - 1, b)
+            for i in range(S):
+                if i in starts:
+                    pe.wait_ge(sem["xa%d" % starts[i]], xin)
+                xpart(b, S - 1 + i, nat(T.xr, i, b))
+                step(b, S - 1 + i, None, prev, nat(T.hs, i, b), True)
+                prev = nat(T.hs, i, b)
+            g.wait_ge(sem["h%d" % b], 2 * S)
+            for dst in (c3, c2):
+                send(dst, nat(T.hl, 0, b), nat(T.hs, S - 1, b), "hi%d" % b, far)
+        sy.wait_ge(sem.snd, tot["snd"])
+        store(0, [S])
+
+    elif core in (c1, c2):
+        dst = c0 if core == c1 else c3
+        mk = topo.mask(core, dst)
+        load_x(XCH)
+        for k, (s0, n) in enumerate(spans(XCH)):
+            g.wait_ge(sem["lx%d" % k], 16)
+            send(dst, cols(T.xr, s0, n), cols(T.xs, s0, n), "xa%d" % k, mk)
+        make_identity()
+        sy.wait_ge(sem.snd, tot["snd"])
+        load_a()
+        pe.wait_ge(sem.idn, 1)
+        for k in range(len(XCH)):
+            pe.wait_ge(sem["lx%d" % k], 16)
+            dv.wait_ge(sem["lx%d" % k], 16)
+        note("hi0", bits(far))
+        if core == c2:
+            note("hi1", bits(far))
+        chain([(T.xs, s) for s in range(S)], [(T.ys, s) for s in range(S)],
+              [nat(T.hl, 0, b) for b in (0, 1)], ["hi0", "hi0" if core == c1 else "hi1"])
+        store(0, YCH)
+
+    else:
+        xin = bits(topo.mask(c2, c3))
+        load_x([S])
+        load_a()
+        make_identity()
+        pe.wait_ge(sem.idn, 1)
+        pe.wait_ge(sem.lx0, 16)
+        dv.wait_ge(sem.lx0, 16)
+        for k in range(len(XCH)):
+            note("xa%d" % k, xin)
+            pe.wait_ge(sem["xa%d" % k], xin)
+            dv.wait_ge(sem["xa%d" % k], xin)
+        note("hi0", bits(far))
+        note("hi1", bits(far))
+        chain([(T.xr, s) for s in range(S)] + [(T.xs, s) for s in range(S)],
+              [(T.hs, s) for s in range(S)] + [(T.ys, s) for s in range(S)],
+              [nat(T.hl, 0, b) for b in (0, 1)], ["hi0", "hi1"])
+        store(S, YCH)
+
+    for b in (0, 1):
+        note("m%d" % b, cm[b])
+        note("z%d" % b, cz[b])
+        note("h%d" % b, ch[b])
+    for name in SEMAPHORES:
+        if tot.get(name, 0) > 0:
+            g.wait_ge(sem[name], tot[name])

@@ -2,8 +2,10 @@ from concourse.mybir import AluOpType, ActivationFunctionType
 
 S, B, H = 8, 128, 64
 XCH = [4, 4]
-YCH = [4, 4]
+YCH = [4, 3, 1]
 NB = 4
+XENG = 16
+HENG = 8
 
 SCRATCH = {
     "xs": ("sbuf", [128, S * B], "bfloat16"),
@@ -14,14 +16,11 @@ SCRATCH = {
     "aw": ("sbuf", [128, 128], "bfloat16"),
     "one": ("sbuf", [128, 128], "bfloat16"),
     "idn": ("sbuf", [128, 128], "bfloat16"),
-    "z0": ("sbuf", [128, H], "float32"),
-    "z1": ("sbuf", [128, H], "float32"),
 }
 for _i in range(2 * NB):
     SCRATCH["p%d" % _i] = ("psum", [128, 512], "float32")
 
-SEMAPHORES = ["lx0", "lx1", "la", "one", "idn", "xa0", "xa1", "hi0", "hi1",
-              "m0", "m1", "z0", "z1", "h0", "h1", "snd", "st"]
+SEMAPHORES = ["lx0", "lx1", "la", "one", "idn", "xa0", "xa1", "hi", "m0", "m1", "h0", "h1", "snd", "st"]
 
 
 def spans(ch):
@@ -32,6 +31,16 @@ def spans(ch):
     return out
 
 
+def low(mask, n):
+    out, e = 0, 0
+    while n > 0:
+        if (mask >> e) & 1:
+            out |= 1 << e
+            n -= 1
+        e += 1
+    return out
+
+
 def rank_program(g, core, T, topo):
     if T.rank_of(core) is None:
         return
@@ -39,9 +48,9 @@ def rank_program(g, core, T, topo):
     if not (topo.may_write(c0, c2) and topo.may_write(c0, c3)):
         raise ValueError("rank 0's core must be allowed to write to ranks 2 and 3")
     sem = T.sem
-    pe, act, dv, sy = g.tensor, g.scalar, g.vector, g.sync
+    pe, act, sy = g.tensor, g.scalar, g.sync
     tot = {}
-    cm, cz, ch = [0, 0], [0, 0], [0, 0]
+    cm, ch = [0, 0], [0, 0]
 
     def note(name, n):
         tot[name] = tot.get(name, 0) + n
@@ -82,47 +91,31 @@ def rank_program(g, core, T, topo):
         act.activation(out, in_, ActivationFunctionType.Tanh).then_inc(sem["h%d" % b], 1)
         ch[b] += 1
 
-    def xpart(b, idx, x):
-        pe.matmul(bank(b, idx), T.idn[:], x, True, False)
-
-    def step(b, idx, x, rhs, out, p, wait=None):
-        ps = bank(b, idx)
-        if wait is None:
-            pe.wait_ge(sem["h%d" % b], ch[b])
-        else:
-            pe.wait_ge(sem[wait], tot[wait])
-        pe.matmul(ps, T.aw[:], rhs, not p, True).then_inc(sem["m%d" % b], 1)
-        cm[b] += 1
-        if p:
-            act.wait_ge(sem["m%d" % b], cm[b])
-            tanh(b, out, ps)
-        else:
-            z = T["z%d" % b][:]
-            dv.wait_ge(sem["m%d" % b], cm[b])
-            dv.tensor_tensor(z, ps, x, AluOpType.add).then_inc(sem["z%d" % b], 1)
-            cz[b] += 1
-            act.wait_ge(sem["z%d" % b], cz[b])
-            tanh(b, out, z)
-
-    def is_p(i):
-        return i < NB or (i - NB) % 3 == 2
-
     def chain(xb, ob, prev, first):
         n = len(xb)
-        x = [[nat(u, s, b) for b in (0, 1)] for u, s in xb]
-        o = [[nat(u, s, b) for b in (0, 1)] for u, s in ob]
-        for i in range(min(NB, n)):
+
+        def xparts(i):
+            u, s, w = xb[i]
+            if w is not None:
+                pe.wait_ge(sem[w], tot[w])
             for b in (0, 1):
-                xpart(b, i, x[i][b])
+                pe.matmul(bank(b, i), T.idn[:], nat(u, s, b), True, False)
+
+        xparts(0)
         pe.wait_ge(sem.la, 16)
         for i in range(n):
             for b in (0, 1):
-                step(b, i, x[i][b], prev[b], o[i][b], is_p(i), first[b] if (i == 0 and first) else None)
-                prev[b] = o[i][b]
-            if NB <= i + 2 < n and is_p(i + 2):
-                xpart(0, i + 2, x[i + 2][0])
-            if NB <= i + 1 < n and is_p(i + 1):
-                xpart(1, i + 1, x[i + 1][1])
+                if i == 0 and first:
+                    pe.wait_ge(sem[first], tot[first])
+                else:
+                    pe.wait_ge(sem["h%d" % b], ch[b])
+                pe.matmul(bank(b, i), T.aw[:], prev[b], False, True).then_inc(sem["m%d" % b], 1)
+                cm[b] += 1
+                act.wait_ge(sem["m%d" % b], cm[b])
+                prev[b] = nat(ob[i][0], ob[i][1], b)
+                tanh(b, prev[b], bank(b, i))
+            if i + 1 < n:
+                xparts(i + 1)
 
     def store(base, chunks):
         for s0, n in spans(chunks):
@@ -131,12 +124,18 @@ def rank_program(g, core, T, topo):
             sy.dma_start(cols(T.y, s0, n), cols(T.ys, s0, n)).then_inc(sem.st, 16)
             note("st", 16)
 
-    dv.memset(T.one[:], 1.0).then_inc(sem.one, 1)
+    def landed(first_only=False):
+        out = []
+        for k, (s0, n) in enumerate(spans(XCH)):
+            note("xa%d" % k, XENG)
+            out += [(T.xr, s0 + j, "xa%d" % k if j == 0 else None) for j in range(n)]
+        return out
+
+    g.vector.memset(T.one[:], 1.0).then_inc(sem.one, 1)
     note("one", 1)
-    far = topo.mask(c0, c3) & topo.mask(c0, c2) & topo.mask(c0, c1)
+    far = low(topo.mask(c0, c3) & topo.mask(c0, c2) & topo.mask(c0, c1), HENG)
 
     if core == c0:
-        xin = bits(topo.mask(c1, c0))
         load_x([1, 7])
         load_a()
         make_identity()
@@ -144,33 +143,22 @@ def rank_program(g, core, T, topo):
         for b in (0, 1):
             tanh(b, nat(T.ys, 0, b), nat(T.xs, 0, b))
         pe.wait_ge(sem.idn, 1)
-        pe.wait_ge(sem.lx1, 16)
-        dv.wait_ge(sem.lx1, 16)
-        chain([(T.xs, s) for s in range(1, S)], [(T.ys, s) for s in range(1, S)],
+        chain([(T.xs, s, "lx1" if s == 1 else None) for s in range(1, S)] + landed(),
+              [(T.ys, s) for s in range(1, S)] + [(T.hs, s) for s in range(S)],
               [nat(T.ys, 0, b) for b in (0, 1)], None)
         for b in (0, 1):
             g.wait_ge(sem["h%d" % b], S)
-        send(c1, T.hl[:], cols(T.ys, S - 1, 1), "hi0", far)
-        starts = {s0: k for k, (s0, n) in enumerate(spans(XCH))}
-        for k in range(len(XCH)):
-            note("xa%d" % k, xin)
+        send(c1, T.hl[:], cols(T.ys, S - 1, 1), "hi", far)
         for b in (0, 1):
-            prev = nat(T.ys, S - 1, b)
-            for i in range(S):
-                if i in starts:
-                    pe.wait_ge(sem["xa%d" % starts[i]], xin)
-                xpart(b, S - 1 + i, nat(T.xr, i, b))
-                step(b, S - 1 + i, None, prev, nat(T.hs, i, b), True)
-                prev = nat(T.hs, i, b)
             g.wait_ge(sem["h%d" % b], 2 * S)
-            for dst in (c3, c2):
-                send(dst, nat(T.hl, 0, b), nat(T.hs, S - 1, b), "hi%d" % b, far)
+        for dst in (c3, c2):
+            send(dst, T.hl[:], cols(T.hs, S - 1, 1), "hi", far)
         sy.wait_ge(sem.snd, tot["snd"])
         store(0, [S])
 
     elif core in (c1, c2):
         dst = c0 if core == c1 else c3
-        mk = topo.mask(core, dst)
+        mk = low(topo.mask(core, dst), XENG)
         load_x(XCH)
         for k, (s0, n) in enumerate(spans(XCH)):
             g.wait_ge(sem["lx%d" % k], 16)
@@ -181,36 +169,24 @@ def rank_program(g, core, T, topo):
         pe.wait_ge(sem.idn, 1)
         for k in range(len(XCH)):
             pe.wait_ge(sem["lx%d" % k], 16)
-            dv.wait_ge(sem["lx%d" % k], 16)
-        note("hi0", bits(far))
-        if core == c2:
-            note("hi1", bits(far))
-        chain([(T.xs, s) for s in range(S)], [(T.ys, s) for s in range(S)],
-              [nat(T.hl, 0, b) for b in (0, 1)], ["hi0", "hi0" if core == c1 else "hi1"])
+        note("hi", bits(far))
+        chain([(T.xs, s, None) for s in range(S)], [(T.ys, s) for s in range(S)],
+              [nat(T.hl, 0, b) for b in (0, 1)], "hi")
         store(0, YCH)
 
     else:
-        xin = bits(topo.mask(c2, c3))
         load_x([S])
         load_a()
         make_identity()
         pe.wait_ge(sem.idn, 1)
-        pe.wait_ge(sem.lx0, 16)
-        dv.wait_ge(sem.lx0, 16)
-        for k in range(len(XCH)):
-            note("xa%d" % k, xin)
-            pe.wait_ge(sem["xa%d" % k], xin)
-            dv.wait_ge(sem["xa%d" % k], xin)
-        note("hi0", bits(far))
-        note("hi1", bits(far))
-        chain([(T.xr, s) for s in range(S)] + [(T.xs, s) for s in range(S)],
+        note("hi", bits(far))
+        chain(landed() + [(T.xs, s, "lx0" if s == 0 else None) for s in range(S)],
               [(T.hs, s) for s in range(S)] + [(T.ys, s) for s in range(S)],
-              [nat(T.hl, 0, b) for b in (0, 1)], ["hi0", "hi1"])
+              [nat(T.hl, 0, b) for b in (0, 1)], "hi")
         store(S, YCH)
 
     for b in (0, 1):
         note("m%d" % b, cm[b])
-        note("z%d" % b, cz[b])
         note("h%d" % b, ch[b])
     for name in SEMAPHORES:
         if tot.get(name, 0) > 0:

@@ -1,9 +1,11 @@
 from concourse.mybir import AluOpType, ActivationFunctionType
 
-S, B, H = 8, 128, 64
+S, B = 8, 128
+BLK = [(0, 32), (32, 32), (64, 32), (96, 32)]
+K = len(BLK)
 XCH = [4, 4]
-YCH = [4, 3, 1]
-NB = 4
+YCH = [4, 2, 1, 1]
+NB = 2
 XENG = 16
 HENG = 8
 
@@ -17,10 +19,11 @@ SCRATCH = {
     "one": ("sbuf", [128, 128], "bfloat16"),
     "idn": ("sbuf", [128, 128], "bfloat16"),
 }
-for _i in range(2 * NB):
+for _i in range(K * NB):
     SCRATCH["p%d" % _i] = ("psum", [128, 512], "float32")
 
-SEMAPHORES = ["lx0", "lx1", "la", "one", "idn", "xa0", "xa1", "hi", "m0", "m1", "h0", "h1", "snd", "st"]
+SEMAPHORES = ["lx0", "lx1", "la", "one", "idn", "xa0", "xa1", "hi", "snd", "st"]
+SEMAPHORES += ["m%d" % _i for _i in range(K)] + ["h%d" % _i for _i in range(K)]
 
 
 def spans(ch):
@@ -49,20 +52,21 @@ def rank_program(g, core, T, topo):
         raise ValueError("rank 0's core must be allowed to write to ranks 2 and 3")
     sem = T.sem
     pe, act, sy = g.tensor, g.scalar, g.sync
+    KS = range(K)
     tot = {}
-    cm, ch = [0, 0], [0, 0]
+    cm, ch = [0] * K, [0] * K
 
     def note(name, n):
         tot[name] = tot.get(name, 0) + n
 
     def nat(buf, s, b):
-        return buf[:, B * s + H * b:B * s + H * b + H]
+        return buf[:, B * s + BLK[b][0]:B * s + BLK[b][0] + BLK[b][1]]
 
     def cols(buf, s0, n):
         return buf[:, B * s0:B * (s0 + n)]
 
     def bank(b, idx):
-        return T["p%d" % (NB * b + idx % NB)][:, 0:H]
+        return T["p%d" % (NB * b + idx % NB)][:, 0:BLK[b][1]]
 
     def bits(m):
         return bin(m).count("1")
@@ -98,13 +102,13 @@ def rank_program(g, core, T, topo):
             u, s, w = xb[i]
             if w is not None:
                 pe.wait_ge(sem[w], tot[w])
-            for b in (0, 1):
+            for b in KS:
                 pe.matmul(bank(b, i), T.idn[:], nat(u, s, b), True, False)
 
         xparts(0)
         pe.wait_ge(sem.la, 16)
         for i in range(n):
-            for b in (0, 1):
+            for b in KS:
                 if i == 0 and first:
                     pe.wait_ge(sem[first], tot[first])
                 else:
@@ -117,14 +121,17 @@ def rank_program(g, core, T, topo):
             if i + 1 < n:
                 xparts(i + 1)
 
+    def wait_states(q, n):
+        for b in KS:
+            q.wait_ge(sem["h%d" % b], n)
+
     def store(base, chunks):
         for s0, n in spans(chunks):
-            for b in (0, 1):
-                sy.wait_ge(sem["h%d" % b], base + s0 + n)
+            wait_states(sy, base + s0 + n)
             sy.dma_start(cols(T.y, s0, n), cols(T.ys, s0, n)).then_inc(sem.st, 16)
             note("st", 16)
 
-    def landed(first_only=False):
+    def landed():
         out = []
         for k, (s0, n) in enumerate(spans(XCH)):
             note("xa%d" % k, XENG)
@@ -140,17 +147,15 @@ def rank_program(g, core, T, topo):
         load_a()
         make_identity()
         act.wait_ge(sem.lx0, 16)
-        for b in (0, 1):
+        for b in KS:
             tanh(b, nat(T.ys, 0, b), nat(T.xs, 0, b))
         pe.wait_ge(sem.idn, 1)
         chain([(T.xs, s, "lx1" if s == 1 else None) for s in range(1, S)] + landed(),
               [(T.ys, s) for s in range(1, S)] + [(T.hs, s) for s in range(S)],
-              [nat(T.ys, 0, b) for b in (0, 1)], None)
-        for b in (0, 1):
-            g.wait_ge(sem["h%d" % b], S)
+              [nat(T.ys, 0, b) for b in KS], None)
+        wait_states(g, S)
         send(c1, T.hl[:], cols(T.ys, S - 1, 1), "hi", far)
-        for b in (0, 1):
-            g.wait_ge(sem["h%d" % b], 2 * S)
+        wait_states(g, 2 * S)
         for dst in (c3, c2):
             send(dst, T.hl[:], cols(T.hs, S - 1, 1), "hi", far)
         sy.wait_ge(sem.snd, tot["snd"])
@@ -171,7 +176,7 @@ def rank_program(g, core, T, topo):
             pe.wait_ge(sem["lx%d" % k], 16)
         note("hi", bits(far))
         chain([(T.xs, s, None) for s in range(S)], [(T.ys, s) for s in range(S)],
-              [nat(T.hl, 0, b) for b in (0, 1)], "hi")
+              [nat(T.hl, 0, b) for b in KS], "hi")
         store(0, YCH)
 
     else:
@@ -182,10 +187,10 @@ def rank_program(g, core, T, topo):
         note("hi", bits(far))
         chain(landed() + [(T.xs, s, "lx0" if s == 0 else None) for s in range(S)],
               [(T.hs, s) for s in range(S)] + [(T.ys, s) for s in range(S)],
-              [nat(T.hl, 0, b) for b in (0, 1)], "hi")
+              [nat(T.hl, 0, b) for b in KS], "hi")
         store(S, YCH)
 
-    for b in (0, 1):
+    for b in KS:
         note("m%d" % b, cm[b])
         note("h%d" % b, ch[b])
     for name in SEMAPHORES:

@@ -4,16 +4,15 @@ S, B = 8, 128
 BLK = [(0, 32), (32, 32), (64, 32), (96, 32)]
 K = len(BLK)
 XCH = [4, 4]
-YCH = [4, 2, 1, 1]
+TAIL = 3
+YCH = {1: [4, 4], 2: [4, 4], 3: [4, S - TAIL - 4]}
 NB = 2
-XENG = 16
-HENG = 8
 
 SCRATCH = {
     "xs": ("sbuf", [128, S * B], "bfloat16"),
-    "xr": ("sbuf", [128, S * B], "bfloat16"),
+    "xr": ("sbuf", [128, 3 * S * B], "bfloat16"),
     "ys": ("sbuf", [128, S * B], "bfloat16"),
-    "hs": ("sbuf", [128, S * B], "bfloat16"),
+    "hs": ("sbuf", [128, 3 * S * B], "bfloat16"),
     "hl": ("sbuf", [128, B], "bfloat16"),
     "aw": ("sbuf", [128, 128], "bfloat16"),
     "one": ("sbuf", [128, 128], "bfloat16"),
@@ -22,7 +21,8 @@ SCRATCH = {
 for _i in range(K * NB):
     SCRATCH["p%d" % _i] = ("psum", [128, 512], "float32")
 
-SEMAPHORES = ["lx0", "lx1", "la", "one", "idn", "xa0", "xa1", "hi", "snd", "st"]
+SEMAPHORES = ["lx0", "lx1", "la", "one", "idn", "hi", "snd", "st"]
+SEMAPHORES += ["xa%d" % _i for _i in range(3 * len(XCH))] + ["ya%d" % _i for _i in range(TAIL)]
 SEMAPHORES += ["m%d" % _i for _i in range(K)] + ["h%d" % _i for _i in range(K)]
 
 
@@ -34,25 +34,17 @@ def spans(ch):
     return out
 
 
-def low(mask, n):
-    out, e = 0, 0
-    while n > 0:
-        if (mask >> e) & 1:
-            out |= 1 << e
-            n -= 1
-        e += 1
-    return out
-
-
 def rank_program(g, core, T, topo):
-    if T.rank_of(core) is None:
+    rank = T.rank_of(core)
+    if rank is None:
         return
     c0, c1, c2, c3 = T.cores
-    if not (topo.may_write(c0, c2) and topo.may_write(c0, c3)):
-        raise ValueError("rank 0's core must be allowed to write to ranks 2 and 3")
+    if not (topo.may_write(c0, c2) and topo.may_write(c0, c3) and topo.may_write(c2, c0)):
+        raise ValueError("ranks 0 and 2 must be allowed to write to each other's chip")
     sem = T.sem
     pe, act, sy = g.tensor, g.scalar, g.sync
     KS = range(K)
+    NX = len(XCH)
     tot = {}
     cm, ch = [0] * K, [0] * K
 
@@ -87,6 +79,8 @@ def rank_program(g, core, T, topo):
         note("la", 16)
 
     def make_identity():
+        g.vector.memset(T.one[:], 1.0).then_inc(sem.one, 1)
+        note("one", 1)
         g.wait_ge(sem.one, 1)
         g.affine_select(T.idn[:], T.one[:], [[-1, 128]], AluOpType.is_equal, 0.0, 0, 1).then_inc(sem.idn, 1)
         note("idn", 1)
@@ -125,24 +119,20 @@ def rank_program(g, core, T, topo):
         for b in KS:
             q.wait_ge(sem["h%d" % b], n)
 
-    def store(base, chunks):
-        for s0, n in spans(chunks):
-            wait_states(sy, base + s0 + n)
-            sy.dma_start(cols(T.y, s0, n), cols(T.ys, s0, n)).then_inc(sem.st, 16)
-            note("st", 16)
+    def put_y(s0, n):
+        sy.dma_start(cols(T.y, s0, n), cols(T.ys, s0, n)).then_inc(sem.st, 16)
+        note("st", 16)
 
-    def landed():
-        out = []
+    def pass_x(r, src_buf, off, dst, waits):
+        mk = topo.mask(core, dst)
         for k, (s0, n) in enumerate(spans(XCH)):
-            note("xa%d" % k, XENG)
-            out += [(T.xr, s0 + j, "xa%d" % k if j == 0 else None) for j in range(n)]
-        return out
+            g.wait_ge(sem[waits[k]], tot[waits[k]])
+            send(dst, cols(T.xr, S * (r - 1) + s0, n), cols(src_buf, off + s0, n), "xa%d" % (NX * (r - 1) + k), mk)
 
-    g.vector.memset(T.one[:], 1.0).then_inc(sem.one, 1)
-    note("one", 1)
-    far = low(topo.mask(c0, c3) & topo.mask(c0, c2) & topo.mask(c0, c1), HENG)
+    far = topo.mask(c0, c3) & topo.mask(c0, c2) & topo.mask(c0, c1)
+    own = ["lx%d" % k for k in range(NX)]
 
-    if core == c0:
+    if rank == 0:
         load_x([1, 7])
         load_a()
         make_identity()
@@ -150,45 +140,58 @@ def rank_program(g, core, T, topo):
         for b in KS:
             tanh(b, nat(T.ys, 0, b), nat(T.xs, 0, b))
         pe.wait_ge(sem.idn, 1)
-        chain([(T.xs, s, "lx1" if s == 1 else None) for s in range(1, S)] + landed(),
-              [(T.ys, s) for s in range(1, S)] + [(T.hs, s) for s in range(S)],
+        xb = [(T.xs, s, "lx1" if s == 1 else None) for s in range(1, S)]
+        for r in (1, 2, 3):
+            for k, (s0, n) in enumerate(spans(XCH)):
+                name = "xa%d" % (NX * (r - 1) + k)
+                note(name, bits(topo.mask(c1 if r == 1 else c2, c0)))
+                xb += [(T.xr, S * (r - 1) + s0 + j, name if j == 0 else None) for j in range(n)]
+        chain(xb, [(T.ys, s) for s in range(1, S)] + [(T.hs, j) for j in range(3 * S)],
               [nat(T.ys, 0, b) for b in KS], None)
         wait_states(g, S)
         send(c1, T.hl[:], cols(T.ys, S - 1, 1), "hi", far)
-        wait_states(g, 2 * S)
-        for dst in (c3, c2):
-            send(dst, T.hl[:], cols(T.hs, S - 1, 1), "hi", far)
-        sy.wait_ge(sem.snd, tot["snd"])
-        store(0, [S])
-
-    elif core in (c1, c2):
-        dst = c0 if core == c1 else c3
-        mk = low(topo.mask(core, dst), XENG)
-        load_x(XCH)
-        for k, (s0, n) in enumerate(spans(XCH)):
-            g.wait_ge(sem["lx%d" % k], 16)
-            send(dst, cols(T.xr, s0, n), cols(T.xs, s0, n), "xa%d" % k, mk)
-        make_identity()
-        sy.wait_ge(sem.snd, tot["snd"])
-        load_a()
-        pe.wait_ge(sem.idn, 1)
-        for k in range(len(XCH)):
-            pe.wait_ge(sem["lx%d" % k], 16)
-        note("hi", bits(far))
-        chain([(T.xs, s, None) for s in range(S)], [(T.ys, s) for s in range(S)],
-              [nat(T.hl, 0, b) for b in KS], "hi")
-        store(0, YCH)
+        wait_states(sy, S)
+        put_y(0, S)
+        for r, dst in ((2, c2), (3, c3)):
+            wait_states(g, S * r)
+            send(dst, T.hl[:], cols(T.hs, S * (r - 1) - 1, 1), "hi", far)
+        for k in range(TAIL):
+            s = S - TAIL + k
+            wait_states(g, 3 * S + s + 1)
+            send(c3, cols(T.ys, s, 1), cols(T.hs, 2 * S + s, 1), "ya%d" % k, far)
 
     else:
-        load_x([S])
+        load_x(XCH)
+        if rank == 1:
+            pass_x(1, T.xs, 0, c0, own)
+            make_identity()
+            sy.wait_ge(sem.snd, tot["snd"])
+        elif rank == 2:
+            pass_x(2, T.xs, 0, c0, own)
+            make_identity()
+            thru = ["xa%d" % (NX * 2 + k) for k in range(NX)]
+            for name in thru:
+                note(name, bits(topo.mask(c3, c2)))
+            pass_x(3, T.xr, S * 2, c0, thru)
+        else:
+            pass_x(3, T.xs, 0, c2, own)
+            make_identity()
         load_a()
-        make_identity()
         pe.wait_ge(sem.idn, 1)
+        for name in own:
+            pe.wait_ge(sem[name], 16)
         note("hi", bits(far))
-        chain(landed() + [(T.xs, s, "lx0" if s == 0 else None) for s in range(S)],
-              [(T.hs, s) for s in range(S)] + [(T.ys, s) for s in range(S)],
+        n_own = sum(YCH[rank])
+        chain([(T.xs, s, None) for s in range(n_own)], [(T.ys, s) for s in range(n_own)],
               [nat(T.hl, 0, b) for b in KS], "hi")
-        store(S, YCH)
+        for s0, n in spans(YCH[rank]):
+            wait_states(sy, s0 + n)
+            put_y(s0, n)
+        if rank == 3:
+            for k in range(TAIL):
+                note("ya%d" % k, bits(far))
+                sy.wait_ge(sem["ya%d" % k], bits(far))
+                put_y(S - TAIL + k, 1)
 
     for b in KS:
         note("m%d" % b, cm[b])

from concourse.mybir import AluOpType, ActivationFunctionType

S, B = 8, 128
BLK = [(0, 32), (32, 32), (64, 32), (96, 32)]
K = len(BLK)
XCH = [4, 4]
TAIL = 3
YCH = {1: [4, 4], 2: [4, 4], 3: [4, S - TAIL - 4]}
NB = 2

SCRATCH = {
    "xs": ("sbuf", [128, S * B], "bfloat16"),
    "xr": ("sbuf", [128, 3 * S * B], "bfloat16"),
    "ys": ("sbuf", [128, S * B], "bfloat16"),
    "hs": ("sbuf", [128, 3 * S * B], "bfloat16"),
    "hl": ("sbuf", [128, B], "bfloat16"),
    "aw": ("sbuf", [128, 128], "bfloat16"),
    "one": ("sbuf", [128, 128], "bfloat16"),
    "idn": ("sbuf", [128, 128], "bfloat16"),
}
for _i in range(K * NB):
    SCRATCH["p%d" % _i] = ("psum", [128, 512], "float32")

SEMAPHORES = ["lx0", "lx1", "la", "one", "idn", "hi", "snd", "st"]
SEMAPHORES += ["xa%d" % _i for _i in range(3 * len(XCH))] + ["ya%d" % _i for _i in range(TAIL)]
SEMAPHORES += ["m%d" % _i for _i in range(K)] + ["h%d" % _i for _i in range(K)]


def spans(ch):
    out, s0 = [], 0
    for n in ch:
        out.append((s0, n))
        s0 += n
    return out


def rank_program(g, core, T, topo):
    rank = T.rank_of(core)
    if rank is None:
        return
    c0, c1, c2, c3 = T.cores
    if not (topo.may_write(c0, c2) and topo.may_write(c0, c3) and topo.may_write(c2, c0)):
        raise ValueError("ranks 0 and 2 must be allowed to write to each other's chip")
    sem = T.sem
    pe, act, sy = g.tensor, g.scalar, g.sync
    KS = range(K)
    NX = len(XCH)
    tot = {}
    cm, ch = [0] * K, [0] * K

    def note(name, n):
        tot[name] = tot.get(name, 0) + n

    def nat(buf, s, b):
        return buf[:, B * s + BLK[b][0]:B * s + BLK[b][0] + BLK[b][1]]

    def cols(buf, s0, n):
        return buf[:, B * s0:B * (s0 + n)]

    def bank(b, idx):
        return T["p%d" % (NB * b + idx % NB)][:, 0:BLK[b][1]]

    def bits(m):
        return bin(m).count("1")

    def send(dst, out_ap, in_ap, rsem, mask):
        rid, pid, se = topo.addr(dst)
        g.remote_dma(out_ap=out_ap, in_ap=in_ap, remote_sem=sem[rsem], local_sem=sem.snd,
                     pid=pid, routing_id=rid, dma_engine_mask=mask)
        note("snd", bits(mask))

    def load_x(chunks):
        for k, (s0, n) in enumerate(spans(chunks)):
            sy.dma_start(cols(T.xs, s0, n), cols(T.x, s0, n)).then_inc(sem["lx%d" % k], 16)
            note("lx%d" % k, 16)

    def load_a():
        sy.dma_start(T.aw[:], T.a[:]).then_inc(sem.la, 16)
        note("la", 16)

    def make_identity():
        g.vector.memset(T.one[:], 1.0).then_inc(sem.one, 1)
        note("one", 1)
        g.wait_ge(sem.one, 1)
        g.affine_select(T.idn[:], T.one[:], [[-1, 128]], AluOpType.is_equal, 0.0, 0, 1).then_inc(sem.idn, 1)
        note("idn", 1)

    def tanh(b, out, in_):
        act.activation(out, in_, ActivationFunctionType.Tanh).then_inc(sem["h%d" % b], 1)
        ch[b] += 1

    def chain(xb, ob, prev, first):
        n = len(xb)

        def xparts(i):
            u, s, w = xb[i]
            if w is not None:
                pe.wait_ge(sem[w], tot[w])
            for b in KS:
                pe.matmul(bank(b, i), T.idn[:], nat(u, s, b), True, False)

        xparts(0)
        pe.wait_ge(sem.la, 16)
        for i in range(n):
            for b in KS:
                if i == 0 and first:
                    pe.wait_ge(sem[first], tot[first])
                else:
                    pe.wait_ge(sem["h%d" % b], ch[b])
                pe.matmul(bank(b, i), T.aw[:], prev[b], False, True).then_inc(sem["m%d" % b], 1)
                cm[b] += 1
                act.wait_ge(sem["m%d" % b], cm[b])
                prev[b] = nat(ob[i][0], ob[i][1], b)
                tanh(b, prev[b], bank(b, i))
            if i + 1 < n:
                xparts(i + 1)

    def wait_states(q, n):
        for b in KS:
            q.wait_ge(sem["h%d" % b], n)

    def put_y(s0, n):
        sy.dma_start(cols(T.y, s0, n), cols(T.ys, s0, n)).then_inc(sem.st, 16)
        note("st", 16)

    def pass_x(r, src_buf, off, dst, waits):
        mk = topo.mask(core, dst)
        for k, (s0, n) in enumerate(spans(XCH)):
            g.wait_ge(sem[waits[k]], tot[waits[k]])
            send(dst, cols(T.xr, S * (r - 1) + s0, n), cols(src_buf, off + s0, n), "xa%d" % (NX * (r - 1) + k), mk)

    far = topo.mask(c0, c3) & topo.mask(c0, c2) & topo.mask(c0, c1)
    own = ["lx%d" % k for k in range(NX)]

    if rank == 0:
        load_x([1, 7])
        load_a()
        make_identity()
        act.wait_ge(sem.lx0, 16)
        for b in KS:
            tanh(b, nat(T.ys, 0, b), nat(T.xs, 0, b))
        pe.wait_ge(sem.idn, 1)
        xb = [(T.xs, s, "lx1" if s == 1 else None) for s in range(1, S)]
        for r in (1, 2, 3):
            for k, (s0, n) in enumerate(spans(XCH)):
                name = "xa%d" % (NX * (r - 1) + k)
                note(name, bits(topo.mask(c1 if r == 1 else c2, c0)))
                xb += [(T.xr, S * (r - 1) + s0 + j, name if j == 0 else None) for j in range(n)]
        chain(xb, [(T.ys, s) for s in range(1, S)] + [(T.hs, j) for j in range(3 * S)],
              [nat(T.ys, 0, b) for b in KS], None)
        wait_states(g, S)
        send(c1, T.hl[:], cols(T.ys, S - 1, 1), "hi", far)
        wait_states(sy, S)
        put_y(0, S)
        for r, dst in ((2, c2), (3, c3)):
            wait_states(g, S * r)
            send(dst, T.hl[:], cols(T.hs, S * (r - 1) - 1, 1), "hi", far)
        for k in range(TAIL):
            s = S - TAIL + k
            wait_states(g, 3 * S + s + 1)
            send(c3, cols(T.ys, s, 1), cols(T.hs, 2 * S + s, 1), "ya%d" % k, far)

    else:
        load_x(XCH)
        if rank == 1:
            pass_x(1, T.xs, 0, c0, own)
            make_identity()
            sy.wait_ge(sem.snd, tot["snd"])
        elif rank == 2:
            pass_x(2, T.xs, 0, c0, own)
            make_identity()
            thru = ["xa%d" % (NX * 2 + k) for k in range(NX)]
            for name in thru:
                note(name, bits(topo.mask(c3, c2)))
            pass_x(3, T.xr, S * 2, c0, thru)
        else:
            pass_x(3, T.xs, 0, c2, own)
            make_identity()
        load_a()
        pe.wait_ge(sem.idn, 1)
        for name in own:
            pe.wait_ge(sem[name], 16)
        note("hi", bits(far))
        n_own = sum(YCH[rank])
        chain([(T.xs, s, None) for s in range(n_own)], [(T.ys, s) for s in range(n_own)],
              [nat(T.hl, 0, b) for b in KS], "hi")
        for s0, n in spans(YCH[rank]):
            wait_states(sy, s0 + n)
            put_y(s0, n)
        if rank == 3:
            for k in range(TAIL):
                note("ya%d" % k, bits(far))
                sy.wait_ge(sem["ya%d" % k], bits(far))
                put_y(S - TAIL + k, 1)

    for b in KS:
        note("m%d" % b, cm[b])
        note("h%d" % b, ch[b])
    for name in SEMAPHORES:
        if tot.get(name, 0) > 0:
            g.wait_ge(sem[name], tot[name])
